import numpy as np, ml_dtypes
CORES = [32,160,288,416,80,208,336,464]
N = 8
R, T = 8192, 1024
HOST = [c // 128 for c in CORES]
G = [[r for r in range(N) if HOST[r] == h] for h in sorted(set(HOST))]
H = len(G); K = [sorted(set(HOST)).index(h) for h in HOST]
def entries(a): return a.T.reshape(-1)
def pack(v, P): return np.ascontiguousarray(np.asarray(v, np.int32).reshape(-1, P).T)
def among(rng, a): return rng.permutation(np.concatenate([a, rng.choice(a, T - len(a))]))
def lists(rng, how):
    O = np.stack([among(rng, np.arange(N)) for g in G])
    if how == "away": O = np.stack([among(rng, [r for r in range(N) if r not in g]) for g in G])
    if how == "home": O = np.stack([among(rng, g) for g in G])
    J = rng.integers(0, R, (H, T)); J[:, rng.integers(T)] = rng.permutation(R)[:H]
    if how == "distinct": O[:], J = rng.integers(N), rng.permutation(R)[:H * T].reshape(H, T)
    if how == "hotrank":
        s = rng.integers(1, H); O[:] = np.array([rng.choice(G[(k + s) % H]) for k in range(H)])[:, None]; J = np.stack([rng.permutation(R)[:T] for g in G])
    I = R * O + J
    if how == "edge":
        C, Q = rng.integers(0, 2 * N, (H, T)), rng.permutation(T)
        C[:, Q[:2 * N]] = np.stack([rng.permutation(2 * N) for g in G]); C[:, Q[2 * N]] = rng.permutation(2 * N)[:H]
        I = R * (C // 2) + (R - 1) * (C % 2)
    return {"idx": np.stack([pack(I[K[r]], 16) for r in range(N)])}
def setup_inputs(rng):
    return dict({"tab": rng.standard_normal((N, 128, R), dtype=np.float32).astype(ml_dtypes.bfloat16)}, **lists(rng, "uniform"))
def setup_inputs_away(rng):
    d = setup_inputs(rng); d.update(lists(rng, "away"))
    for k in ("tab",): d[k] = (d[k].astype(np.float32) * 1048576.0).astype(d[k].dtype)
    return d
def setup_inputs_distinct(rng):
    d = setup_inputs(rng); d.update(lists(rng, "distinct"))
    for k in ("tab",): d[k] = (d[k].astype(np.float32) * (1 / 1024.0)).astype(d[k].dtype)
    return d
def setup_inputs_edge(rng):
    d = setup_inputs(rng); d.update(lists(rng, "edge"))
    return d
def setup_inputs_home(rng):
    d = setup_inputs(rng); d.update(lists(rng, "home"))
    return d
def setup_inputs_hotrank(rng):
    d = setup_inputs(rng); d.update(lists(rng, "hotrank"))
    return d
def check_inputs(x):
    bad = []
    if x["idx"].min() < 0 or x["idx"].max() >= N * R: bad.append("idx out of range")
    if any((x["idx"][r] != x["idx"][s]).any() for r in range(N) for s in range(r) if HOST[r] == HOST[s]): bad.append("two ranks of one host hold different lists")
    return bad
def reference(tab, idx):
    A = np.concatenate(list(tab), axis=1)
    return {"y": np.stack([A[:, entries(idx[r])] for r in range(N)])}

@@ -1,0 +1,283 @@
+from concourse.bass import DstId, RemoteDMATransfer
+from concourse.mybir import AluOpType, ActivationFunctionType
+
+R = 8192
+NT = 1024
+HF = 512
+QT = 256
+NCH = 4
+
+SCRATCH = {
+    "win": ("sbuf", [128, R + 3 * HF], "bfloat16"),
+    "stage": ("sbuf", [128, 7 * HF], "bfloat16"),
+    "fin": ("sbuf", [128, 2 * NT], "bfloat16"),
+    "yb": ("sbuf", [128, NT], "bfloat16"),
+    "an": ("sbuf", [128, 4 * 64], "int32"), "ow": ("sbuf", [128, 64], "int32"),
+    "rhs": ("sbuf", [128, 4 * 160], "float32"),
+    "tmp": ("sbuf", [128, 16 * 64], "float32"),
+    "jj": ("sbuf", [128, 64], "float32"), "ph": ("sbuf", [128, 32], "float32"),
+    "ones": ("sbuf", [128, 128], "float32"), "sel": ("sbuf", [128, 128], "float32"),
+    "mp": ("dram", [128, 4], "int32"),
+    "mx": ("sbuf", [128, 32], "int32"), "mo": ("sbuf", [128, 16], "int32"),
+    "mi": ("sbuf", [128, 16], "int32"), "mk": ("sbuf", [128, 16], "int32"), "mc": ("sbuf", [128, 16], "float32"),
+    "mt": ("sbuf", [128, 6 * 16], "float32"), "moff": ("sbuf", [128, 16], "uint16"),
+    "mwin": ("sbuf", [128, 4 * QT], "bfloat16"), "mout": ("sbuf", [128, QT], "bfloat16"),
+}
+for _n in "opdr":
+    SCRATCH["x" + _n] = ("sbuf", [128, 64], "int32")
+    SCRATCH["off" + _n] = ("sbuf", [128, 160], "uint16")
+    SCRATCH["ps" + _n] = ("psum", [128, 512], "float32")
+    SCRATCH["l%sa" % _n] = SCRATCH["l%sb" % _n] = ("dram", [128, 4], "int32")
+SEMAPHORES = (["si", "lp", "ld", "lr", "ls", "gi", "vm", "v1", "v2", "v3", "v4", "v5",
+               "sP", "sD", "sO", "sR", "rk", "rm", "ag", "cb", "fv", "fs", "st",
+               "ml", "mx", "mg", "m1", "m2", "m3", "m4", "marr", "mw"]
+              + [k + n for k in ("x", "p", "off", "c1", "c2") for n in "opdr"] + ["tb%d" % i for i in range(NCH)])
+
+COPY = ActivationFunctionType.Copy
+A = AluOpType
+
+
+def bits(mask):
+    return [1 << i for i in range(32) if mask >> i & 1]
+
+
+def parts(mask, n):
+    b = bits(mask)
+    k = len(b) // n
+    return [sum(b[i * k:(i + 1) * k]) for i in range(n)]
+
+
+def mergers(x, topo):
+    near = [y for y in range(max(0, x - 16), x + 16) if y != x and topo.host(y) == topo.host(x) and topo.chip(y) == topo.chip(x)]
+    return [[y for y in near if topo.die(y) == topo.die(x)][0], [y for y in near if topo.die(y) != topo.die(x)][0]]
+
+
+def place(x, T, topo):
+    C = list(T.cores)
+    host = [y for y in C if topo.host(y) == topo.host(x)]
+    rack = [y for y in C if topo.rack(topo.host(y)) == topo.rack(topo.host(x))]
+    other = [y for y in rack if topo.host(y) != topo.host(x)]
+    cable = [y for y in C if y not in rack and topo.may_write(x, y)]
+    return {"hi": host.index(x), "mate": [y for y in host if y != x][0], "rack": rack, "other": other, "cable": cable,
+            "twin": [y for y in other if topo.chip(y) == topo.chip(x)][0],
+            "far": [y for y in cable if topo.chip(y) == topo.chip(x)][0],
+            "foreign": [y for y in C if y not in rack]}
+
+
+def tr(topo, src, dsts, outs, in_, mask, sem):
+    ids = []
+    for d in dsts:
+        rid, pid = topo.addr(d, src)
+        ids.append(DstId(rid=rid, pnc=pid))
+    return RemoteDMATransfer(srcs=[in_], dsts=list(outs), dst_ids=ids, dma_engine_mask=mask, remote_sem=sem)
+
+
+def rank_core(g, x, T, topo):
+    s = T.sem
+    me = place(x, T, topo)
+    hi, mate, twin, far, oth = me["hi"], me["mate"], me["twin"], me["far"], me["other"]
+    M = mergers(x, topo)
+    off8 = topo.mask(x, mate)
+    on8 = topo.mask(x, M[0]) & ~off8
+    sent = [0]
+
+    def fused(*ts):
+        g.remote_dma_fused([tr(topo, x, *a) for a in ts], local_sem=s.ls)
+        sent[0] += sum(len(bits(a[3])) for a in ts)
+
+    V, S, Y, P = g.vector, g.scalar, g.sync, g.tensor
+
+    S.dma_start(T.loa[:], T.idx[:, 0:32]).then_inc(s.si, 16)
+    Y.dma_start(T.lob[:], T.idx[:, 32:64]).then_inc(s.si, 16)
+    S.dma_start(T.xo[0:16, :], T.idx[:]).then_inc(s.xo, 16)
+    w = R // NCH
+    for i in range(NCH):
+        if i >= 2:
+            Y.wait_ge(s["tb%d" % (i - 2)], 16)
+        Y.dma_start(T.win[:, i * w:(i + 1) * w], T.tab[:, i * w:(i + 1) * w]).then_inc(s["tb%d" % i], 16)
+    for n, cnt in (("p", 8), ("d", 8), ("r", 16)):
+        Y.wait_ge(s["l" + n], cnt)
+        for k in (0, 1):
+            Y.dma_start(T["x" + n][0:16, 32 * k:32 * k + 32], T["l" + n + "ab"[k]][:]).then_inc(s["x" + n], 16)
+
+    V.memset(T.ones[0:16, :], 1.0).then_inc(s.vm, 1)
+    g.iota(T.jj[0:16, :], [[16, 64]], 0, 1, allow_small_or_imprecise_dtypes=True).then_inc(s.gi, 1)
+    g.iota(T.ph[0:16, :], [[16, 32]], 0, 1, allow_small_or_imprecise_dtypes=True).then_inc(s.gi, 1)
+    g.wait_ge(s.vm, 1)
+    g.affine_select(T.sel[0:16, :], T.ones[0:16, :], [[0, 8], [-1, 16]], A.is_equal, 0.0, 0, 1).then_inc(s.gi, 1)
+
+    m2, m4, o2 = parts(off8, 2), parts(off8, 4), parts(on8, 2)
+    g.wait_ge(s.si, 32)
+    fused(([far, M[0]], [T.lpa[:], T.loa[:]], T.loa[:], m2[0], s.lp),
+          ([far, M[1]], [T.lpb[:], T.loa[:]], T.lob[:], m2[1], s.lp))
+    g.wait_ge(s.lp, 8)
+    fused(([twin], [T.lda[:]], T.lpa[:], m2[0], s.ld), ([twin], [T.ldb[:]], T.lpb[:], m2[1], s.ld))
+    fused((M, [T.mp[:], T.mp[:]], (T.lpa, T.lpb)[hi][:], on8, s.ml))
+
+    def blk(i, a=0, b=HF):
+        return T.stage[:, i * HF + a:i * HF + b]
+
+    def to_mergers(dst, b, m):
+        k = place(dst, T, topo)["rack"].index(x)
+        D = mergers(dst, topo)
+        return [([D[i]], [T.mwin[:, k * QT:(k + 1) * QT]], blk(b, i * QT, (i + 1) * QT), m[i], s.marr) for i in (0, 1)]
+
+    def to_rank(dst, b, m):
+        k = R + [y for y in place(dst, T, topo)["rack"] if y != dst].index(x) * HF
+        return ([dst], [T.win[:, k:k + HF]], blk(b), m, s.rk)
+    g.wait_ge(s.sP, 2)
+    fused(*(to_mergers(mate, 0, m2) + to_mergers(x, 1, o2)))
+    g.wait_ge(s.sD, 2)
+    fused(*(to_mergers(oth[0], 2, m4[0:2]) + to_mergers(oth[1], 3, m4[2:4])))
+    g.wait_ge(s.sO, 2)
+    fused(to_rank(mate, 6, off8))
+    g.wait_ge(s.sR, 2)
+    fused(to_rank(oth[0], 4, m2[0]), to_rank(oth[1], 5, m2[1]))
+    own = T.fin[:, hi * HF:(hi + 1) * HF]
+    g.wait_ge(s.rm, 2)
+    fused(([mate], [own], own, off8, s.ag))
+    g.wait_ge(s.ls, sent[0])
+    g.wait_ge(s.st, 32)
+
+    H = slice(hi * 32, hi * 32 + 32)
+    q16 = slice(0, 16)
+
+    def tmp(i, n):
+        return T.tmp[q16, i * 64:i * 64 + n]
+
+    def ts(o, a, c1, c2, sem):
+        V.tensor_scalar(o, a, float(c1), float(c2), A.is_equal, A.mult).then_inc(sem, 1)
+
+    def tt(o, a, b, op, sem):
+        V.tensor_tensor(o, a, b, op).then_inc(sem, 1)
+    V.wait_ge(s.xo, 16)
+    V.wait_ge(s.gi, 3)
+    V.tensor_scalar(T.an[q16, 0:64], T.xo[q16, :], R - 1, None, A.bitwise_and).then_inc(s.v1, 1)
+    V.tensor_scalar(T.ow[q16, :], T.xo[q16, :], R.bit_length() - 1, None, A.arith_shift_right).then_inc(s.v1, 1)
+    V.wait_ge(s.v1, 2)
+    V.tensor_copy(T.rhs[q16, 0:64], T.an[q16, 0:64]).then_inc(s.v2, 1)
+    for i, y in enumerate(me["foreign"]):
+        ts(tmp(i, 64), T.ow[q16, :], T.rank_of(y), NT, s.v2)
+    for i, y in enumerate([y for y in me["rack"] if y != x]):
+        ts(tmp(4 + i, 32), T.ow[q16, H], T.rank_of(y), R + i * HF, s.v2)
+    ts(tmp(7, 32), T.ow[q16, H], T.rank_of(x), 1, s.v2)
+    V.wait_ge(s.v2, 9)
+    tt(tmp(8, 64), tmp(0, 64), tmp(1, 64), A.add, s.v3)
+    tt(tmp(9, 64), tmp(2, 64), tmp(3, 64), A.add, s.v3)
+    tt(tmp(10, 32), tmp(4, 32), tmp(5, 32), A.add, s.v3)
+    tt(tmp(11, 32), tmp(6, 32), T.ph[q16, :], A.add, s.v3)
+    tt(tmp(12, 32), T.rhs[q16, H], T.ph[q16, :], A.subtract, s.v3)
+    V.wait_ge(s.v3, 5)
+    tt(tmp(13, 64), tmp(8, 64), tmp(9, 64), A.add, s.v4)
+    tt(tmp(14, 32), tmp(10, 32), tmp(11, 32), A.add, s.v4)
+    tt(tmp(15, 32), tmp(7, 32), tmp(12, 32), A.mult, s.v4)
+    V.wait_ge(s.v4, 3)
+    tt(T.rhs[q16, 64:96], tmp(14, 32), tmp(15, 32), A.add, s.v5)
+    tt(T.rhs[q16, 96:160], tmp(13, 64), T.jj[q16, :], A.add, s.v5)
+    P.wait_ge(s.gi, 3)
+    P.wait_ge(s.v2, 9)
+    P.wait_ge(s.v5, 2)
+    P.matmul(T.pso[:, 0:160], T.sel[q16, :], T.rhs[q16, 0:160], True, True).then_inc(s.po, 1)
+    V.wait_ge(s.po, 1)
+    V.tensor_copy(T.offo[:], T.pso[:, 0:160]).then_inc(s.offo, 1)
+
+    def conv(k, n):
+        a, f = T.an[q16, k * 64:(k + 1) * 64], T.rhs[q16, k * 160:k * 160 + 64]
+        V.wait_ge(s["x" + n], 32)
+        V.tensor_scalar(a, T["x" + n][q16, :], R - 1, None, A.bitwise_and).then_inc(s["c1" + n], 1)
+        V.wait_ge(s["c1" + n], 1)
+        V.tensor_copy(f, a).then_inc(s["c2" + n], 1)
+        P.wait_ge(s["c2" + n], 1)
+        P.matmul(T["ps" + n][:, 0:64], T.sel[q16, :], f, True, True).then_inc(s["p" + n], 1)
+        V.wait_ge(s["p" + n], 1)
+        V.tensor_copy(T["off" + n][:, 0:64], T["ps" + n][:, 0:64]).then_inc(s["off" + n], 1)
+
+    def pair(n, ov, cv, os, cs, sem, win, k=32):
+        off = T["off" + n]
+        for q in (V, S):
+            q.wait_ge(s["off" + n], 1)
+        V.tensor_copy(ov, win.indirect(off[:, cv:cv + k])).then_inc(sem, 1)
+        S.activation(os, win.indirect(off[:, cs:cs + k]), COPY).then_inc(sem, 1)
+    tabw = T.win[:, 0:R]
+    h0, h1 = [place(y, T, topo)["hi"] * 32 for y in oth]
+    conv(1, "p")
+    for q in (V, S):
+        for i in range(NCH):
+            q.wait_ge(s["tb%d" % i], 16)
+    pair("p", blk(0), 32 - hi * 32, blk(1), hi * 32, s.sP, tabw)
+    conv(2, "d")
+    pair("d", blk(2), h0, blk(3), h1, s.sD, tabw)
+    c = 32 - hi * 32
+    pair("o", blk(6, 0, QT), c, blk(6, QT, HF), c + 16, s.sO, tabw, 16)
+    conv(3, "r")
+    pair("r", blk(4), h0, blk(5), h1, s.sR, tabw)
+    for q in (V, S):
+        q.wait_ge(s.rk, 16)
+    pair("o", T.fin[:, hi * HF:hi * HF + QT], 64, T.fin[:, hi * HF + QT:(hi + 1) * HF], 80, s.rm, T.win[:], 16)
+    for q in (V, S):
+        q.wait_ge(s.rm, 2)
+        q.wait_ge(s.ag, 8)
+        q.wait_ge(s.cb, 32)
+    V.tensor_copy(T.yb[:, 0:HF], T.fin[:].indirect(T.offo[:, 96:128])).then_inc(s.fv, 1)
+    S.activation(T.yb[:, HF:NT], T.fin[:].indirect(T.offo[:, 128:160]), COPY).then_inc(s.fs, 1)
+    Y.wait_ge(s.fv, 1)
+    Y.dma_start(T.y[:, 0:HF], T.yb[:, 0:HF]).then_inc(s.st, 16)
+    S.wait_ge(s.fs, 1)
+    S.dma_start(T.y[:, HF:NT], T.yb[:, HF:NT]).then_inc(s.st, 16)
+
+
+def merger_core(g, m, x, k, T, topo):
+    s = T.sem
+    me = place(x, T, topo)
+    twin, hi = me["twin"], me["hi"]
+    V, S, Y = g.vector, g.scalar, g.sync
+    off8 = topo.mask(m, twin)
+    g.iota(T.mi[:], [[0, 16]], 0, 1).then_inc(s.mg, 1)
+    g.iota(T.mc[:], [[16, 16]], 0, 0, allow_small_or_imprecise_dtypes=True).then_inc(s.mg, 1)
+    g.wait_ge(s.lp, 4)
+    rid, pid = topo.addr(twin, m)
+    g.remote_dma((T.lra, T.lrb)[k][:], T.loa[:], s.lr, s.ls, pid=pid, routing_id=rid, dma_engine_mask=off8)
+
+    Y.wait_ge(s.ml, 8)
+    for i in range(8):
+        Y.dma_start(T.mx[16 * i:16 * i + 16, :], T.mp[:]).then_inc(s.mx, 16)
+    V.wait_ge(s.mx, 128)
+    V.wait_ge(s.mg, 2)
+    V.tensor_scalar(T.mo[:], T.mx[:, 16 * k:16 * k + 16], R.bit_length() - 1, None, A.arith_shift_right).then_inc(s.m1, 1)
+    V.tensor_scalar(T.mk[:], T.mi[:], 15, None, A.bitwise_and).then_inc(s.m1, 1)
+    V.wait_ge(s.m1, 2)
+
+    def mt(i):
+        return T.mt[:, 16 * i:16 * i + 16]
+    for i, y in enumerate(me["rack"][1:]):
+        V.tensor_scalar(mt(i), T.mo[:], float(T.rank_of(y)), float(QT * (i + 1)), A.is_equal, A.mult).then_inc(s.m2, 1)
+    V.tensor_tensor(mt(3), T.mk[:], T.mc[:], A.add).then_inc(s.m2, 1)
+    V.wait_ge(s.m2, 4)
+    V.tensor_tensor(mt(4), mt(0), mt(1), A.add).then_inc(s.m3, 1)
+    V.tensor_tensor(mt(5), mt(2), mt(3), A.add).then_inc(s.m3, 1)
+    V.wait_ge(s.m3, 2)
+    V.tensor_tensor(mt(0), mt(4), mt(5), A.add).then_inc(s.m3, 1)
+    V.wait_ge(s.m3, 3)
+    V.tensor_copy(T.moff[:], mt(0)).then_inc(s.m4, 1)
+
+    for q in (V, S):
+        q.wait_ge(s.m4, 1)
+        q.wait_ge(s.marr, 12)
+    V.tensor_copy(T.mout[:, 0:128], T.mwin[:].indirect(T.moff[:, 0:8])).then_inc(s.mw, 1)
+    S.activation(T.mout[:, 128:QT], T.mwin[:].indirect(T.moff[:, 8:16]), COPY).then_inc(s.mw, 1)
+    g.wait_ge(s.mw, 2)
+    c = NT + hi * HF + k * QT
+    o = T.fin[:, c:c + QT]
+    far = me["cable"]
+    g.remote_dma_fused([tr(topo, m, far, [o for _ in far], T.mout[:], off8, s.cb)], local_sem=s.ls)
+    g.wait_ge(s.ls, 2 * len(bits(off8)))
+
+
+def rank_program(g, core, T, topo):
+    if T.rank_of(core) is not None:
+        return rank_core(g, core, T, topo)
+    for x in T.cores:
+        if topo.host(x) == topo.host(core) and topo.chip(x) == topo.chip(core):
+            M = mergers(x, topo)
+            if core in M:
+                merger_core(g, core, x, M.index(core), T, topo)

@@ -8,30 +8,26 @@ QT = 256
 NCH = 4
 
 SCRATCH = {
-    "win": ("sbuf", [128, R + 3 * HF], "bfloat16"),
+    "win": ("sbuf", [128, R + 4 * HF], "bfloat16"),
     "stage": ("sbuf", [128, 7 * HF], "bfloat16"),
-    "fin": ("sbuf", [128, 2 * NT], "bfloat16"),
     "yb": ("sbuf", [128, NT], "bfloat16"),
-    "an": ("sbuf", [128, 4 * 64], "int32"), "ow": ("sbuf", [128, 64], "int32"),
-    "rhs": ("sbuf", [128, 4 * 160], "float32"),
-    "tmp": ("sbuf", [128, 16 * 64], "float32"),
-    "jj": ("sbuf", [128, 64], "float32"), "ph": ("sbuf", [128, 32], "float32"),
-    "ones": ("sbuf", [128, 128], "float32"), "sel": ("sbuf", [128, 128], "float32"),
-    "mp": ("dram", [128, 4], "int32"),
-    "mx": ("sbuf", [128, 32], "int32"), "mo": ("sbuf", [128, 16], "int32"),
+    "xo": ("sbuf", [128, 64], "int32"),
+    "an": ("sbuf", [128, 32], "int32"), "ow": ("sbuf", [128, 32], "int32"),
+    "ri": ("sbuf", [128, 32], "int32"), "rm": ("sbuf", [128, 32], "int32"), "rc": ("sbuf", [128, 32], "float32"),
+    "tmp": ("sbuf", [128, 12 * 32], "float32"), "offh": ("sbuf", [128, 32], "uint16"),
+    "mp": ("sbuf", [128, 32], "uint16"), "mh": ("sbuf", [128, 32], "uint16"),
+    "mx": ("sbuf", [128, 16], "int32"), "mo": ("sbuf", [128, 16], "int32"),
     "mi": ("sbuf", [128, 16], "int32"), "mk": ("sbuf", [128, 16], "int32"), "mc": ("sbuf", [128, 16], "float32"),
     "mt": ("sbuf", [128, 6 * 16], "float32"), "moff": ("sbuf", [128, 16], "uint16"),
     "mwin": ("sbuf", [128, 4 * QT], "bfloat16"), "mout": ("sbuf", [128, QT], "bfloat16"),
+    "rl": ("sbuf", [128, 3 * HF], "bfloat16"),
 }
 for _n in "opdr":
-    SCRATCH["x" + _n] = ("sbuf", [128, 64], "int32")
-    SCRATCH["off" + _n] = ("sbuf", [128, 160], "uint16")
-    SCRATCH["ps" + _n] = ("psum", [128, 512], "float32")
-    SCRATCH["l%sa" % _n] = SCRATCH["l%sb" % _n] = ("dram", [128, 4], "int32")
-SEMAPHORES = (["si", "lp", "ld", "lr", "ls", "gi", "vm", "v1", "v2", "v3", "v4", "v5",
-               "sP", "sD", "sO", "sR", "rk", "rm", "ag", "cb", "fv", "fs", "st",
-               "ml", "mx", "mg", "m1", "m2", "m3", "m4", "marr", "mw"]
-              + [k + n for k in ("x", "p", "off", "c1", "c2") for n in "opdr"] + ["tb%d" % i for i in range(NCH)])
+    SCRATCH["l" + _n] = SCRATCH["off" + _n] = ("sbuf", [128, 64], "uint16")
+SEMAPHORES = (["xo", "lo", "lp", "ld", "lr", "ls", "gi", "v1", "v2", "v3", "v4", "v5", "v6", "oh",
+               "sP", "sD0", "sD1", "sO", "sR", "rk", "ag0", "ag1", "cb0", "cb1", "fin0", "fin1", "st", "q0", "q1", "q2",
+               "ml", "mh", "mx", "mg", "m1", "m2", "m3", "m4", "marr", "mw"]
+              + ["off" + n for n in "opdr"] + ["tb%d" % i for i in range(NCH)])
 
 COPY = ActivationFunctionType.Copy
 A = AluOpType
@@ -47,9 +43,11 @@ def parts(mask, n):
     return [sum(b[i * k:(i + 1) * k]) for i in range(n)]
 
 
-def mergers(x, topo):
+def helpers(x, topo):
     near = [y for y in range(max(0, x - 16), x + 16) if y != x and topo.host(y) == topo.host(x) and topo.chip(y) == topo.chip(x)]
-    return [[y for y in near if topo.die(y) == topo.die(x)][0], [y for y in near if topo.die(y) != topo.die(x)][0]]
+    same = [y for y in near if topo.die(y) == topo.die(x)]
+    other = [y for y in near if topo.die(y) != topo.die(x)]
+    return [same[0], other[0]], other[1]
 
 
 def place(x, T, topo):
@@ -58,10 +56,16 @@ def place(x, T, topo):
     rack = [y for y in C if topo.rack(topo.host(y)) == topo.rack(topo.host(x))]
     other = [y for y in rack if topo.host(y) != topo.host(x)]
     cable = [y for y in C if y not in rack and topo.may_write(x, y)]
-    return {"hi": host.index(x), "mate": [y for y in host if y != x][0], "rack": rack, "other": other, "cable": cable,
+    hi = host.index(x)
+    return {"hi": hi, "mate": [y for y in host if y != x][0], "rack": rack, "other": other,
+            "direct": other[hi], "relayed": other[1 - hi],
             "twin": [y for y in other if topo.chip(y) == topo.chip(x)][0],
-            "far": [y for y in cable if topo.chip(y) == topo.chip(x)][0],
-            "foreign": [y for y in C if y not in rack]}
+            "far": [y for y in cable if topo.chip(y) == topo.chip(x)][0]}
+
+
+def slot(dst, x, T, topo):
+    k = R + [y for y in place(dst, T, topo)["rack"] if y != dst].index(x) * HF
+    return T.win[:, k:k + HF]
 
 
 def tr(topo, src, dsts, outs, in_, mask, sem):
@@ -72,179 +76,174 @@ def tr(topo, src, dsts, outs, in_, mask, sem):
     return RemoteDMATransfer(srcs=[in_], dsts=list(outs), dst_ids=ids, dma_engine_mask=mask, remote_sem=sem)
 
 
+def to_merger(dst, i, x, buf, at, mask, T, topo):
+    k = place(dst, T, topo)["rack"].index(x)
+    return ([helpers(dst, topo)[0][i]], [T.mwin[:, k * QT:(k + 1) * QT]], buf[:, at:at + QT], mask, T.sem.marr)
+
+
 def rank_core(g, x, T, topo):
     s = T.sem
     me = place(x, T, topo)
     hi, mate, twin, far, oth = me["hi"], me["mate"], me["twin"], me["far"], me["other"]
-    M = mergers(x, topo)
+    M, relay = helpers(x, topo)
     off8 = topo.mask(x, mate)
     on8 = topo.mask(x, M[0]) & ~off8
+    m2, o2 = parts(off8, 2), parts(on8, 2)
+    n8 = len(bits(off8))
     sent = [0]
 
     def fused(*ts):
         g.remote_dma_fused([tr(topo, x, *a) for a in ts], local_sem=s.ls)
         sent[0] += sum(len(bits(a[3])) for a in ts)
 
-    V, S, Y, P = g.vector, g.scalar, g.sync, g.tensor
+    V, S, Y = g.vector, g.scalar, g.sync
 
-    S.dma_start(T.loa[:], T.idx[:, 0:32]).then_inc(s.si, 16)
-    Y.dma_start(T.lob[:], T.idx[:, 32:64]).then_inc(s.si, 16)
-    S.dma_start(T.xo[0:16, :], T.idx[:]).then_inc(s.xo, 16)
+    for i in range(8):
+        (S, Y)[i % 2].dma_start(T.xo[16 * i:16 * i + 16, :], T.idx[:]).then_inc(s.xo, 16)
     w = R // NCH
     for i in range(NCH):
         if i >= 2:
             Y.wait_ge(s["tb%d" % (i - 2)], 16)
         Y.dma_start(T.win[:, i * w:(i + 1) * w], T.tab[:, i * w:(i + 1) * w]).then_inc(s["tb%d" % i], 16)
-    for n, cnt in (("p", 8), ("d", 8), ("r", 16)):
-        Y.wait_ge(s["l" + n], cnt)
-        for k in (0, 1):
-            Y.dma_start(T["x" + n][0:16, 32 * k:32 * k + 32], T["l" + n + "ab"[k]][:]).then_inc(s["x" + n], 16)
 
-    V.memset(T.ones[0:16, :], 1.0).then_inc(s.vm, 1)
-    g.iota(T.jj[0:16, :], [[16, 64]], 0, 1, allow_small_or_imprecise_dtypes=True).then_inc(s.gi, 1)
-    g.iota(T.ph[0:16, :], [[16, 32]], 0, 1, allow_small_or_imprecise_dtypes=True).then_inc(s.gi, 1)
-    g.wait_ge(s.vm, 1)
-    g.affine_select(T.sel[0:16, :], T.ones[0:16, :], [[0, 8], [-1, 16]], A.is_equal, 0.0, 0, 1).then_inc(s.gi, 1)
-
-    m2, m4, o2 = parts(off8, 2), parts(off8, 4), parts(on8, 2)
-    g.wait_ge(s.si, 32)
-    fused(([far, M[0]], [T.lpa[:], T.loa[:]], T.loa[:], m2[0], s.lp),
-          ([far, M[1]], [T.lpb[:], T.loa[:]], T.lob[:], m2[1], s.lp))
-    g.wait_ge(s.lp, 8)
-    fused(([twin], [T.lda[:]], T.lpa[:], m2[0], s.ld), ([twin], [T.ldb[:]], T.lpb[:], m2[1], s.ld))
-    fused((M, [T.mp[:], T.mp[:]], (T.lpa, T.lpb)[hi][:], on8, s.ml))
+    g.iota(T.ri[:], [[0, 32]], 0, 1).then_inc(s.gi, 1)
+    g.iota(T.rc[:], [[16, 32]], 0, 0, allow_small_or_imprecise_dtypes=True).then_inc(s.gi, 1)
+    g.wait_ge(s.lo, 1)
+    fused(([far], [T.lp[:]], T.lo[:], off8, s.lp))
+    fused(*[([(M[0], relay)[k]], [T.mh[:]], T.lo[:, 32 * k:32 * k + 32], o2[k], s.mh) for k in (0, 1)])
+    g.wait_ge(s.lp, n8)
+    fused(([twin], [T.ld[:]], T.lp[:], off8, s.ld))
+    fused(([M[1]], [T.mp[:]], T.lp[:, 32 * hi:32 * hi + 32], on8, s.ml))
 
     def blk(i, a=0, b=HF):
         return T.stage[:, i * HF + a:i * HF + b]
-
-    def to_mergers(dst, b, m):
-        k = place(dst, T, topo)["rack"].index(x)
-        D = mergers(dst, topo)
-        return [([D[i]], [T.mwin[:, k * QT:(k + 1) * QT]], blk(b, i * QT, (i + 1) * QT), m[i], s.marr) for i in (0, 1)]
-
-    def to_rank(dst, b, m):
-        k = R + [y for y in place(dst, T, topo)["rack"] if y != dst].index(x) * HF
-        return ([dst], [T.win[:, k:k + HF]], blk(b), m, s.rk)
+    di, ri = oth.index(me["direct"]), oth.index(me["relayed"])
     g.wait_ge(s.sP, 2)
-    fused(*(to_mergers(mate, 0, m2) + to_mergers(x, 1, o2)))
-    g.wait_ge(s.sD, 2)
-    fused(*(to_mergers(oth[0], 2, m4[0:2]) + to_mergers(oth[1], 3, m4[2:4])))
+    fused(*([([relay], [T.rl[:, i * QT:(i + 1) * QT]], blk(0, i * QT, (i + 1) * QT), m2[i], s.q0) for i in (0, 1)]
+            + [to_merger(x, i, x, T.stage, HF + i * QT, o2[i], T, topo) for i in (0, 1)]))
+    for i in (0, 1):
+        g.wait_ge(s["sD%d" % i], 2)
+        fused(*[to_merger(oth[j], i, x, T.stage, (2 + j) * HF + i * QT, m2[j], T, topo) for j in (0, 1)])
     g.wait_ge(s.sO, 2)
-    fused(to_rank(mate, 6, off8))
+    fused(([relay], [T.rl[:, HF:2 * HF]], blk(6), on8, s.q1))
     g.wait_ge(s.sR, 2)
-    fused(to_rank(oth[0], 4, m2[0]), to_rank(oth[1], 5, m2[1]))
-    own = T.fin[:, hi * HF:(hi + 1) * HF]
-    g.wait_ge(s.rm, 2)
-    fused(([mate], [own], own, off8, s.ag))
+    fused(([me["direct"]], [slot(me["direct"], x, T, topo)], blk(4 + di), off8, s.rk),
+          ([relay], [T.rl[:, 2 * HF:3 * HF]], blk(4 + ri), on8, s.q2))
+    own, his = hi * HF, HF - hi * HF
+    for i in (0, 1):
+        q = T.yb[:, own + i * QT:own + (i + 1) * QT]
+        g.wait_ge(s["fin%d" % i], 2)
+        fused(([mate], [q], q, off8, s["ag%d" % i]))
     g.wait_ge(s.ls, sent[0])
-    g.wait_ge(s.st, 32)
+    g.wait_ge(s.st, 48)
 
-    H = slice(hi * 32, hi * 32 + 32)
-    q16 = slice(0, 16)
+    mine = R * T.rank_of(x)
 
-    def tmp(i, n):
-        return T.tmp[q16, i * 64:i * 64 + n]
+    def conv(n, src):
+        V.tensor_scalar(T["off" + n][:], src, float(mine), float(R - 1), A.subtract, A.min).then_inc(s["off" + n], 1)
 
-    def ts(o, a, c1, c2, sem):
-        V.tensor_scalar(o, a, float(c1), float(c2), A.is_equal, A.mult).then_inc(sem, 1)
+    def tmp(i):
+        return T.tmp[:, i * 32:i * 32 + 32]
 
     def tt(o, a, b, op, sem):
         V.tensor_tensor(o, a, b, op).then_inc(sem, 1)
-    V.wait_ge(s.xo, 16)
-    V.wait_ge(s.gi, 3)
-    V.tensor_scalar(T.an[q16, 0:64], T.xo[q16, :], R - 1, None, A.bitwise_and).then_inc(s.v1, 1)
-    V.tensor_scalar(T.ow[q16, :], T.xo[q16, :], R.bit_length() - 1, None, A.arith_shift_right).then_inc(s.v1, 1)
-    V.wait_ge(s.v1, 2)
-    V.tensor_copy(T.rhs[q16, 0:64], T.an[q16, 0:64]).then_inc(s.v2, 1)
-    for i, y in enumerate(me["foreign"]):
-        ts(tmp(i, 64), T.ow[q16, :], T.rank_of(y), NT, s.v2)
+    V.wait_ge(s.xo, 128)
+    V.tensor_copy(T.lo[:], T.xo[:]).then_inc(s.lo, 1)
+    conv("o", T.xo[:])
+    own_x = T.xo[:, hi * 32:hi * 32 + 32]
+    V.tensor_scalar(T.an[:], own_x, R - 1, None, A.bitwise_and).then_inc(s.v1, 1)
+    V.tensor_scalar(T.ow[:], own_x, R.bit_length() - 1, None, A.arith_shift_right).then_inc(s.v1, 1)
+    V.wait_ge(s.gi, 2)
+    V.tensor_scalar(T.rm[:], T.ri[:], 15, None, A.bitwise_and).then_inc(s.v1, 1)
+    V.wait_ge(s.v1, 3)
     for i, y in enumerate([y for y in me["rack"] if y != x]):
-        ts(tmp(4 + i, 32), T.ow[q16, H], T.rank_of(y), R + i * HF, s.v2)
-    ts(tmp(7, 32), T.ow[q16, H], T.rank_of(x), 1, s.v2)
-    V.wait_ge(s.v2, 9)
-    tt(tmp(8, 64), tmp(0, 64), tmp(1, 64), A.add, s.v3)
-    tt(tmp(9, 64), tmp(2, 64), tmp(3, 64), A.add, s.v3)
-    tt(tmp(10, 32), tmp(4, 32), tmp(5, 32), A.add, s.v3)
-    tt(tmp(11, 32), tmp(6, 32), T.ph[q16, :], A.add, s.v3)
-    tt(tmp(12, 32), T.rhs[q16, H], T.ph[q16, :], A.subtract, s.v3)
-    V.wait_ge(s.v3, 5)
-    tt(tmp(13, 64), tmp(8, 64), tmp(9, 64), A.add, s.v4)
-    tt(tmp(14, 32), tmp(10, 32), tmp(11, 32), A.add, s.v4)
-    tt(tmp(15, 32), tmp(7, 32), tmp(12, 32), A.mult, s.v4)
-    V.wait_ge(s.v4, 3)
-    tt(T.rhs[q16, 64:96], tmp(14, 32), tmp(15, 32), A.add, s.v5)
-    tt(T.rhs[q16, 96:160], tmp(13, 64), T.jj[q16, :], A.add, s.v5)
-    P.wait_ge(s.gi, 3)
-    P.wait_ge(s.v2, 9)
-    P.wait_ge(s.v5, 2)
-    P.matmul(T.pso[:, 0:160], T.sel[q16, :], T.rhs[q16, 0:160], True, True).then_inc(s.po, 1)
-    V.wait_ge(s.po, 1)
-    V.tensor_copy(T.offo[:], T.pso[:, 0:160]).then_inc(s.offo, 1)
+        V.tensor_scalar(tmp(i), T.ow[:], float(T.rank_of(y)), float((i - 3) * HF), A.is_equal, A.mult).then_inc(s.v2, 1)
+    V.tensor_scalar(tmp(3), T.ow[:], float(T.rank_of(x)), None, A.is_equal).then_inc(s.v2, 1)
+    tt(tmp(4), T.rm[:], T.rc[:], A.add, s.v2)
+    V.wait_ge(s.v2, 5)
+    tt(tmp(5), tmp(0), tmp(1), A.add, s.v3)
+    V.tensor_scalar(tmp(6), tmp(4), float(R + 3 * HF), None, A.add).then_inc(s.v3, 1)
+    V.wait_ge(s.v3, 2)
+    tt(tmp(7), tmp(5), tmp(2), A.add, s.v4)
+    tt(tmp(8), T.an[:], tmp(6), A.subtract, s.v4)
+    V.wait_ge(s.v4, 2)
+    tt(tmp(9), tmp(7), tmp(6), A.add, s.v5)
+    tt(tmp(10), tmp(3), tmp(8), A.mult, s.v5)
+    V.wait_ge(s.v5, 2)
+    tt(tmp(11), tmp(9), tmp(10), A.add, s.v6)
+    V.wait_ge(s.v6, 1)
+    V.tensor_copy(T.offh[:], tmp(11)).then_inc(s.oh, 1)
+    V.wait_ge(s.lp, n8)
+    conv("p", T.lp[:])
 
-    def conv(k, n):
-        a, f = T.an[q16, k * 64:(k + 1) * 64], T.rhs[q16, k * 160:k * 160 + 64]
-        V.wait_ge(s["x" + n], 32)
-        V.tensor_scalar(a, T["x" + n][q16, :], R - 1, None, A.bitwise_and).then_inc(s["c1" + n], 1)
-        V.wait_ge(s["c1" + n], 1)
-        V.tensor_copy(f, a).then_inc(s["c2" + n], 1)
-        P.wait_ge(s["c2" + n], 1)
-        P.matmul(T["ps" + n][:, 0:64], T.sel[q16, :], f, True, True).then_inc(s["p" + n], 1)
-        V.wait_ge(s["p" + n], 1)
-        V.tensor_copy(T["off" + n][:, 0:64], T["ps" + n][:, 0:64]).then_inc(s["off" + n], 1)
-
-    def pair(n, ov, cv, os, cs, sem, win, k=32):
-        off = T["off" + n]
+    def pair(off, osem, ov, cv, os, cs, sem, win, k=32):
         for q in (V, S):
-            q.wait_ge(s["off" + n], 1)
+            q.wait_ge(osem, 1)
         V.tensor_copy(ov, win.indirect(off[:, cv:cv + k])).then_inc(sem, 1)
         S.activation(os, win.indirect(off[:, cs:cs + k]), COPY).then_inc(sem, 1)
     tabw = T.win[:, 0:R]
     h0, h1 = [place(y, T, topo)["hi"] * 32 for y in oth]
-    conv(1, "p")
+    c = 32 - hi * 32
     for q in (V, S):
         for i in range(NCH):
             q.wait_ge(s["tb%d" % i], 16)
-    pair("p", blk(0), 32 - hi * 32, blk(1), hi * 32, s.sP, tabw)
-    conv(2, "d")
-    pair("d", blk(2), h0, blk(3), h1, s.sD, tabw)
-    c = 32 - hi * 32
-    pair("o", blk(6, 0, QT), c, blk(6, QT, HF), c + 16, s.sO, tabw, 16)
-    conv(3, "r")
-    pair("r", blk(4), h0, blk(5), h1, s.sR, tabw)
-    for q in (V, S):
-        q.wait_ge(s.rk, 16)
-    pair("o", T.fin[:, hi * HF:hi * HF + QT], 64, T.fin[:, hi * HF + QT:(hi + 1) * HF], 80, s.rm, T.win[:], 16)
-    for q in (V, S):
-        q.wait_ge(s.rm, 2)
-        q.wait_ge(s.ag, 8)
-        q.wait_ge(s.cb, 32)
-    V.tensor_copy(T.yb[:, 0:HF], T.fin[:].indirect(T.offo[:, 96:128])).then_inc(s.fv, 1)
-    S.activation(T.yb[:, HF:NT], T.fin[:].indirect(T.offo[:, 128:160]), COPY).then_inc(s.fs, 1)
-    Y.wait_ge(s.fv, 1)
-    Y.dma_start(T.y[:, 0:HF], T.yb[:, 0:HF]).then_inc(s.st, 16)
-    S.wait_ge(s.fs, 1)
-    S.dma_start(T.y[:, HF:NT], T.yb[:, HF:NT]).then_inc(s.st, 16)
+    pair(T.offp, s.offp, blk(0), c, blk(1), hi * 32, s.sP, tabw)
+    V.wait_ge(s.ld, n8)
+    conv("d", T.ld[:])
+    for i in (0, 1):
+        a, b = i * QT, (i + 1) * QT
+        pair(T.offd, s.offd, blk(2, a, b), h0 + 16 * i, blk(3, a, b), h1 + 16 * i, s["sD%d" % i], tabw, 16)
+    pair(T.offo, s.offo, blk(6, 0, QT), c, blk(6, QT, HF), c + 16, s.sO, tabw, 16)
+    V.wait_ge(s.lr, 2 * n8)
+    conv("r", T.lr[:])
+    pair(T.offr, s.offr, blk(4), h0, blk(5), h1, s.sR, tabw)
+    for i in (0, 1):
+        for q in (V, S):
+            if i == 0:
+                q.wait_ge(s.rk, 3 * n8)
+            else:
+                pass
+            q.wait_ge(s["cb%d" % i], n8)
+        a = own + i * QT
+        W = T.win[:, 0:R + 3 * HF + (i + 1) * QT]
+        pair(T.offh, s.oh, T.yb[:, a:a + 128], 16 * i, T.yb[:, a + 128:a + QT], 16 * i + 8, s["fin%d" % i], W, 8)
+    for i in (0, 1):
+        S.wait_ge(s["fin%d" % i], 2)
+    S.dma_start(T.y[:, own:own + HF], T.yb[:, own:own + HF]).then_inc(s.st, 16)
+    for i in (0, 1):
+        a = his + i * QT
+        Y.wait_ge(s["ag%d" % i], n8)
+        Y.dma_start(T.y[:, a:a + QT], T.yb[:, a:a + QT]).then_inc(s.st, 16)
+
+
+def pass_list(g, q, k, T, topo, twin):
+    s = T.sem
+    g.wait_ge(s.mh, 4)
+    g.remote_dma_fused([tr(topo, q, [twin], [T.lr[:, 32 * k:32 * k + 32]], T.mh[:], topo.mask(q, twin), s.lr)], local_sem=s.ls)
 
 
 def merger_core(g, m, x, k, T, topo):
     s = T.sem
     me = place(x, T, topo)
-    twin, hi = me["twin"], me["hi"]
-    V, S, Y = g.vector, g.scalar, g.sync
+    twin, far = me["twin"], me["far"]
+    M = helpers(x, topo)[0]
+    V, S = g.vector, g.scalar
     off8 = topo.mask(m, twin)
+    n8 = len(bits(off8))
     g.iota(T.mi[:], [[0, 16]], 0, 1).then_inc(s.mg, 1)
     g.iota(T.mc[:], [[16, 16]], 0, 0, allow_small_or_imprecise_dtypes=True).then_inc(s.mg, 1)
-    g.wait_ge(s.lp, 4)
-    rid, pid = topo.addr(twin, m)
-    g.remote_dma((T.lra, T.lrb)[k][:], T.loa[:], s.lr, s.ls, pid=pid, routing_id=rid, dma_engine_mask=off8)
+    if k == 0:
+        pass_list(g, m, 0, T, topo, twin)
+    else:
+        g.wait_ge(s.ml, 8)
+        g.remote_dma_fused([tr(topo, m, [M[0]], [T.mp[:]], T.mp[:], off8, s.ml)], local_sem=s.ls)
 
-    Y.wait_ge(s.ml, 8)
-    for i in range(8):
-        Y.dma_start(T.mx[16 * i:16 * i + 16, :], T.mp[:]).then_inc(s.mx, 16)
-    V.wait_ge(s.mx, 128)
     V.wait_ge(s.mg, 2)
-    V.tensor_scalar(T.mo[:], T.mx[:, 16 * k:16 * k + 16], R.bit_length() - 1, None, A.arith_shift_right).then_inc(s.m1, 1)
     V.tensor_scalar(T.mk[:], T.mi[:], 15, None, A.bitwise_and).then_inc(s.m1, 1)
+    V.wait_ge(s.ml, 8)
+    V.tensor_copy(T.mx[:], T.mp[:, 16 * k:16 * k + 16]).then_inc(s.mx, 1)
+    V.wait_ge(s.mx, 1)
+    V.tensor_scalar(T.mo[:], T.mx[:], R.bit_length() - 1, None, A.arith_shift_right).then_inc(s.m1, 1)
     V.wait_ge(s.m1, 2)
 
     def mt(i):
@@ -262,15 +261,29 @@ def merger_core(g, m, x, k, T, topo):
 
     for q in (V, S):
         q.wait_ge(s.m4, 1)
-        q.wait_ge(s.marr, 12)
+        q.wait_ge(s.marr, 16)
     V.tensor_copy(T.mout[:, 0:128], T.mwin[:].indirect(T.moff[:, 0:8])).then_inc(s.mw, 1)
     S.activation(T.mout[:, 128:QT], T.mwin[:].indirect(T.moff[:, 8:16]), COPY).then_inc(s.mw, 1)
     g.wait_ge(s.mw, 2)
-    c = NT + hi * HF + k * QT
-    o = T.fin[:, c:c + QT]
-    far = me["cable"]
-    g.remote_dma_fused([tr(topo, m, far, [o for _ in far], T.mout[:], off8, s.cb)], local_sem=s.ls)
-    g.wait_ge(s.ls, 2 * len(bits(off8)))
+    c = R + 3 * HF + k * QT
+    g.remote_dma_fused([tr(topo, m, [far], [T.win[:, c:c + QT]], T.mout[:], off8, s["cb%d" % k])], local_sem=s.ls)
+    g.wait_ge(s.ls, 2 * n8)
+
+
+def relay_core(g, q, x, T, topo):
+    s = T.sem
+    me = place(x, T, topo)
+    mate = me["mate"]
+    off8 = topo.mask(q, mate)
+    n8, m2 = len(bits(off8)), parts(off8, 2)
+    pass_list(g, q, 1, T, topo, me["twin"])
+    g.wait_ge(s.q0, 8)
+    g.remote_dma_fused([tr(topo, q, *to_merger(mate, i, x, T.rl, i * QT, m2[i], T, topo)) for i in (0, 1)], local_sem=s.ls)
+    for i, y in ((1, mate), (2, me["relayed"])):
+        g.wait_ge(s["q%d" % i], 8)
+        g.remote_dma_fused([tr(topo, q, [y], [slot(y, x, T, topo)], T.rl[:, i * HF:(i + 1) * HF], off8, s.rk)],
+                           local_sem=s.ls)
+    g.wait_ge(s.ls, 4 * n8)
 
 
 def rank_program(g, core, T, topo):
@@ -278,6 +291,8 @@ def rank_program(g, core, T, topo):
         return rank_core(g, core, T, topo)
     for x in T.cores:
         if topo.host(x) == topo.host(core) and topo.chip(x) == topo.chip(core):
-            M = mergers(x, topo)
+            M, relay = helpers(x, topo)
             if core in M:
                 merger_core(g, core, x, M.index(core), T, topo)
+            elif core == relay:
+                relay_core(g, core, x, T, topo)

from concourse.bass import DstId, RemoteDMATransfer
from concourse.mybir import AluOpType, ActivationFunctionType

R = 8192
NT = 1024
HF = 512
QT = 256
NCH = 4

SCRATCH = {
    "win": ("sbuf", [128, R + 4 * HF], "bfloat16"),
    "stage": ("sbuf", [128, 7 * HF], "bfloat16"),
    "yb": ("sbuf", [128, NT], "bfloat16"),
    "xo": ("sbuf", [128, 64], "int32"),
    "an": ("sbuf", [128, 32], "int32"), "ow": ("sbuf", [128, 32], "int32"),
    "ri": ("sbuf", [128, 32], "int32"), "rm": ("sbuf", [128, 32], "int32"), "rc": ("sbuf", [128, 32], "float32"),
    "tmp": ("sbuf", [128, 12 * 32], "float32"), "offh": ("sbuf", [128, 32], "uint16"),
    "mp": ("sbuf", [128, 32], "uint16"), "mh": ("sbuf", [128, 32], "uint16"),
    "mx": ("sbuf", [128, 16], "int32"), "mo": ("sbuf", [128, 16], "int32"),
    "mi": ("sbuf", [128, 16], "int32"), "mk": ("sbuf", [128, 16], "int32"), "mc": ("sbuf", [128, 16], "float32"),
    "mt": ("sbuf", [128, 6 * 16], "float32"), "moff": ("sbuf", [128, 16], "uint16"),
    "mwin": ("sbuf", [128, 4 * QT], "bfloat16"), "mout": ("sbuf", [128, QT], "bfloat16"),
    "rl": ("sbuf", [128, 3 * HF], "bfloat16"),
}
for _n in "opdr":
    SCRATCH["l" + _n] = SCRATCH["off" + _n] = ("sbuf", [128, 64], "uint16")
SEMAPHORES = (["xo", "lo", "lp", "ld", "lr", "ls", "gi", "v1", "v2", "v3", "v4", "v5", "v6", "oh",
               "sP", "sD0", "sD1", "sO", "sR", "rk", "ag0", "ag1", "cb0", "cb1", "fin0", "fin1", "st", "q0", "q1", "q2",
               "ml", "mh", "mx", "mg", "m1", "m2", "m3", "m4", "marr", "mw"]
              + ["off" + n for n in "opdr"] + ["tb%d" % i for i in range(NCH)])

COPY = ActivationFunctionType.Copy
A = AluOpType


def bits(mask):
    return [1 << i for i in range(32) if mask >> i & 1]


def parts(mask, n):
    b = bits(mask)
    k = len(b) // n
    return [sum(b[i * k:(i + 1) * k]) for i in range(n)]


def helpers(x, topo):
    near = [y for y in range(max(0, x - 16), x + 16) if y != x and topo.host(y) == topo.host(x) and topo.chip(y) == topo.chip(x)]
    same = [y for y in near if topo.die(y) == topo.die(x)]
    other = [y for y in near if topo.die(y) != topo.die(x)]
    return [same[0], other[0]], other[1]


def place(x, T, topo):
    C = list(T.cores)
    host = [y for y in C if topo.host(y) == topo.host(x)]
    rack = [y for y in C if topo.rack(topo.host(y)) == topo.rack(topo.host(x))]
    other = [y for y in rack if topo.host(y) != topo.host(x)]
    cable = [y for y in C if y not in rack and topo.may_write(x, y)]
    hi = host.index(x)
    return {"hi": hi, "mate": [y for y in host if y != x][0], "rack": rack, "other": other,
            "direct": other[hi], "relayed": other[1 - hi],
            "twin": [y for y in other if topo.chip(y) == topo.chip(x)][0],
            "far": [y for y in cable if topo.chip(y) == topo.chip(x)][0]}


def slot(dst, x, T, topo):
    k = R + [y for y in place(dst, T, topo)["rack"] if y != dst].index(x) * HF
    return T.win[:, k:k + HF]


def tr(topo, src, dsts, outs, in_, mask, sem):
    ids = []
    for d in dsts:
        rid, pid = topo.addr(d, src)
        ids.append(DstId(rid=rid, pnc=pid))
    return RemoteDMATransfer(srcs=[in_], dsts=list(outs), dst_ids=ids, dma_engine_mask=mask, remote_sem=sem)


def to_merger(dst, i, x, buf, at, mask, T, topo):
    k = place(dst, T, topo)["rack"].index(x)
    return ([helpers(dst, topo)[0][i]], [T.mwin[:, k * QT:(k + 1) * QT]], buf[:, at:at + QT], mask, T.sem.marr)


def rank_core(g, x, T, topo):
    s = T.sem
    me = place(x, T, topo)
    hi, mate, twin, far, oth = me["hi"], me["mate"], me["twin"], me["far"], me["other"]
    M, relay = helpers(x, topo)
    off8 = topo.mask(x, mate)
    on8 = topo.mask(x, M[0]) & ~off8
    m2, o2 = parts(off8, 2), parts(on8, 2)
    n8 = len(bits(off8))
    sent = [0]

    def fused(*ts):
        g.remote_dma_fused([tr(topo, x, *a) for a in ts], local_sem=s.ls)
        sent[0] += sum(len(bits(a[3])) for a in ts)

    V, S, Y = g.vector, g.scalar, g.sync

    for i in range(8):
        (S, Y)[i % 2].dma_start(T.xo[16 * i:16 * i + 16, :], T.idx[:]).then_inc(s.xo, 16)
    w = R // NCH
    for i in range(NCH):
        if i >= 2:
            Y.wait_ge(s["tb%d" % (i - 2)], 16)
        Y.dma_start(T.win[:, i * w:(i + 1) * w], T.tab[:, i * w:(i + 1) * w]).then_inc(s["tb%d" % i], 16)

    g.iota(T.ri[:], [[0, 32]], 0, 1).then_inc(s.gi, 1)
    g.iota(T.rc[:], [[16, 32]], 0, 0, allow_small_or_imprecise_dtypes=True).then_inc(s.gi, 1)
    g.wait_ge(s.lo, 1)
    fused(([far], [T.lp[:]], T.lo[:], off8, s.lp))
    fused(*[([(M[0], relay)[k]], [T.mh[:]], T.lo[:, 32 * k:32 * k + 32], o2[k], s.mh) for k in (0, 1)])
    g.wait_ge(s.lp, n8)
    fused(([twin], [T.ld[:]], T.lp[:], off8, s.ld))
    fused(([M[1]], [T.mp[:]], T.lp[:, 32 * hi:32 * hi + 32], on8, s.ml))

    def blk(i, a=0, b=HF):
        return T.stage[:, i * HF + a:i * HF + b]
    di, ri = oth.index(me["direct"]), oth.index(me["relayed"])
    g.wait_ge(s.sP, 2)
    fused(*([([relay], [T.rl[:, i * QT:(i + 1) * QT]], blk(0, i * QT, (i + 1) * QT), m2[i], s.q0) for i in (0, 1)]
            + [to_merger(x, i, x, T.stage, HF + i * QT, o2[i], T, topo) for i in (0, 1)]))
    for i in (0, 1):
        g.wait_ge(s["sD%d" % i], 2)
        fused(*[to_merger(oth[j], i, x, T.stage, (2 + j) * HF + i * QT, m2[j], T, topo) for j in (0, 1)])
    g.wait_ge(s.sO, 2)
    fused(([relay], [T.rl[:, HF:2 * HF]], blk(6), on8, s.q1))
    g.wait_ge(s.sR, 2)
    fused(([me["direct"]], [slot(me["direct"], x, T, topo)], blk(4 + di), off8, s.rk),
          ([relay], [T.rl[:, 2 * HF:3 * HF]], blk(4 + ri), on8, s.q2))
    own, his = hi * HF, HF - hi * HF
    for i in (0, 1):
        q = T.yb[:, own + i * QT:own + (i + 1) * QT]
        g.wait_ge(s["fin%d" % i], 2)
        fused(([mate], [q], q, off8, s["ag%d" % i]))
    g.wait_ge(s.ls, sent[0])
    g.wait_ge(s.st, 48)

    mine = R * T.rank_of(x)

    def conv(n, src):
        V.tensor_scalar(T["off" + n][:], src, float(mine), float(R - 1), A.subtract, A.min).then_inc(s["off" + n], 1)

    def tmp(i):
        return T.tmp[:, i * 32:i * 32 + 32]

    def tt(o, a, b, op, sem):
        V.tensor_tensor(o, a, b, op).then_inc(sem, 1)
    V.wait_ge(s.xo, 128)
    V.tensor_copy(T.lo[:], T.xo[:]).then_inc(s.lo, 1)
    conv("o", T.xo[:])
    own_x = T.xo[:, hi * 32:hi * 32 + 32]
    V.tensor_scalar(T.an[:], own_x, R - 1, None, A.bitwise_and).then_inc(s.v1, 1)
    V.tensor_scalar(T.ow[:], own_x, R.bit_length() - 1, None, A.arith_shift_right).then_inc(s.v1, 1)
    V.wait_ge(s.gi, 2)
    V.tensor_scalar(T.rm[:], T.ri[:], 15, None, A.bitwise_and).then_inc(s.v1, 1)
    V.wait_ge(s.v1, 3)
    for i, y in enumerate([y for y in me["rack"] if y != x]):
        V.tensor_scalar(tmp(i), T.ow[:], float(T.rank_of(y)), float((i - 3) * HF), A.is_equal, A.mult).then_inc(s.v2, 1)
    V.tensor_scalar(tmp(3), T.ow[:], float(T.rank_of(x)), None, A.is_equal).then_inc(s.v2, 1)
    tt(tmp(4), T.rm[:], T.rc[:], A.add, s.v2)
    V.wait_ge(s.v2, 5)
    tt(tmp(5), tmp(0), tmp(1), A.add, s.v3)
    V.tensor_scalar(tmp(6), tmp(4), float(R + 3 * HF), None, A.add).then_inc(s.v3, 1)
    V.wait_ge(s.v3, 2)
    tt(tmp(7), tmp(5), tmp(2), A.add, s.v4)
    tt(tmp(8), T.an[:], tmp(6), A.subtract, s.v4)
    V.wait_ge(s.v4, 2)
    tt(tmp(9), tmp(7), tmp(6), A.add, s.v5)
    tt(tmp(10), tmp(3), tmp(8), A.mult, s.v5)
    V.wait_ge(s.v5, 2)
    tt(tmp(11), tmp(9), tmp(10), A.add, s.v6)
    V.wait_ge(s.v6, 1)
    V.tensor_copy(T.offh[:], tmp(11)).then_inc(s.oh, 1)
    V.wait_ge(s.lp, n8)
    conv("p", T.lp[:])

    def pair(off, osem, ov, cv, os, cs, sem, win, k=32):
        for q in (V, S):
            q.wait_ge(osem, 1)
        V.tensor_copy(ov, win.indirect(off[:, cv:cv + k])).then_inc(sem, 1)
        S.activation(os, win.indirect(off[:, cs:cs + k]), COPY).then_inc(sem, 1)
    tabw = T.win[:, 0:R]
    h0, h1 = [place(y, T, topo)["hi"] * 32 for y in oth]
    c = 32 - hi * 32
    for q in (V, S):
        for i in range(NCH):
            q.wait_ge(s["tb%d" % i], 16)
    pair(T.offp, s.offp, blk(0), c, blk(1), hi * 32, s.sP, tabw)
    V.wait_ge(s.ld, n8)
    conv("d", T.ld[:])
    for i in (0, 1):
        a, b = i * QT, (i + 1) * QT
        pair(T.offd, s.offd, blk(2, a, b), h0 + 16 * i, blk(3, a, b), h1 + 16 * i, s["sD%d" % i], tabw, 16)
    pair(T.offo, s.offo, blk(6, 0, QT), c, blk(6, QT, HF), c + 16, s.sO, tabw, 16)
    V.wait_ge(s.lr, 2 * n8)
    conv("r", T.lr[:])
    pair(T.offr, s.offr, blk(4), h0, blk(5), h1, s.sR, tabw)
    for i in (0, 1):
        for q in (V, S):
            if i == 0:
                q.wait_ge(s.rk, 3 * n8)
            else:
                pass
            q.wait_ge(s["cb%d" % i], n8)
        a = own + i * QT
        W = T.win[:, 0:R + 3 * HF + (i + 1) * QT]
        pair(T.offh, s.oh, T.yb[:, a:a + 128], 16 * i, T.yb[:, a + 128:a + QT], 16 * i + 8, s["fin%d" % i], W, 8)
    for i in (0, 1):
        S.wait_ge(s["fin%d" % i], 2)
    S.dma_start(T.y[:, own:own + HF], T.yb[:, own:own + HF]).then_inc(s.st, 16)
    for i in (0, 1):
        a = his + i * QT
        Y.wait_ge(s["ag%d" % i], n8)
        Y.dma_start(T.y[:, a:a + QT], T.yb[:, a:a + QT]).then_inc(s.st, 16)


def pass_list(g, q, k, T, topo, twin):
    s = T.sem
    g.wait_ge(s.mh, 4)
    g.remote_dma_fused([tr(topo, q, [twin], [T.lr[:, 32 * k:32 * k + 32]], T.mh[:], topo.mask(q, twin), s.lr)], local_sem=s.ls)


def merger_core(g, m, x, k, T, topo):
    s = T.sem
    me = place(x, T, topo)
    twin, far = me["twin"], me["far"]
    M = helpers(x, topo)[0]
    V, S = g.vector, g.scalar
    off8 = topo.mask(m, twin)
    n8 = len(bits(off8))
    g.iota(T.mi[:], [[0, 16]], 0, 1).then_inc(s.mg, 1)
    g.iota(T.mc[:], [[16, 16]], 0, 0, allow_small_or_imprecise_dtypes=True).then_inc(s.mg, 1)
    if k == 0:
        pass_list(g, m, 0, T, topo, twin)
    else:
        g.wait_ge(s.ml, 8)
        g.remote_dma_fused([tr(topo, m, [M[0]], [T.mp[:]], T.mp[:], off8, s.ml)], local_sem=s.ls)

    V.wait_ge(s.mg, 2)
    V.tensor_scalar(T.mk[:], T.mi[:], 15, None, A.bitwise_and).then_inc(s.m1, 1)
    V.wait_ge(s.ml, 8)
    V.tensor_copy(T.mx[:], T.mp[:, 16 * k:16 * k + 16]).then_inc(s.mx, 1)
    V.wait_ge(s.mx, 1)
    V.tensor_scalar(T.mo[:], T.mx[:], R.bit_length() - 1, None, A.arith_shift_right).then_inc(s.m1, 1)
    V.wait_ge(s.m1, 2)

    def mt(i):
        return T.mt[:, 16 * i:16 * i + 16]
    for i, y in enumerate(me["rack"][1:]):
        V.tensor_scalar(mt(i), T.mo[:], float(T.rank_of(y)), float(QT * (i + 1)), A.is_equal, A.mult).then_inc(s.m2, 1)
    V.tensor_tensor(mt(3), T.mk[:], T.mc[:], A.add).then_inc(s.m2, 1)
    V.wait_ge(s.m2, 4)
    V.tensor_tensor(mt(4), mt(0), mt(1), A.add).then_inc(s.m3, 1)
    V.tensor_tensor(mt(5), mt(2), mt(3), A.add).then_inc(s.m3, 1)
    V.wait_ge(s.m3, 2)
    V.tensor_tensor(mt(0), mt(4), mt(5), A.add).then_inc(s.m3, 1)
    V.wait_ge(s.m3, 3)
    V.tensor_copy(T.moff[:], mt(0)).then_inc(s.m4, 1)

    for q in (V, S):
        q.wait_ge(s.m4, 1)
        q.wait_ge(s.marr, 16)
    V.tensor_copy(T.mout[:, 0:128], T.mwin[:].indirect(T.moff[:, 0:8])).then_inc(s.mw, 1)
    S.activation(T.mout[:, 128:QT], T.mwin[:].indirect(T.moff[:, 8:16]), COPY).then_inc(s.mw, 1)
    g.wait_ge(s.mw, 2)
    c = R + 3 * HF + k * QT
    g.remote_dma_fused([tr(topo, m, [far], [T.win[:, c:c + QT]], T.mout[:], off8, s["cb%d" % k])], local_sem=s.ls)
    g.wait_ge(s.ls, 2 * n8)


def relay_core(g, q, x, T, topo):
    s = T.sem
    me = place(x, T, topo)
    mate = me["mate"]
    off8 = topo.mask(q, mate)
    n8, m2 = len(bits(off8)), parts(off8, 2)
    pass_list(g, q, 1, T, topo, me["twin"])
    g.wait_ge(s.q0, 8)
    g.remote_dma_fused([tr(topo, q, *to_merger(mate, i, x, T.rl, i * QT, m2[i], T, topo)) for i in (0, 1)], local_sem=s.ls)
    for i, y in ((1, mate), (2, me["relayed"])):
        g.wait_ge(s["q%d" % i], 8)
        g.remote_dma_fused([tr(topo, q, [y], [slot(y, x, T, topo)], T.rl[:, i * HF:(i + 1) * HF], off8, s.rk)],
                           local_sem=s.ls)
    g.wait_ge(s.ls, 4 * n8)


def rank_program(g, core, T, topo):
    if T.rank_of(core) is not None:
        return rank_core(g, core, T, topo)
    for x in T.cores:
        if topo.host(x) == topo.host(core) and topo.chip(x) == topo.chip(core):
            M, relay = helpers(x, topo)
            if core in M:
                merger_core(g, core, x, M.index(core), T, topo)
            elif core == relay:
                relay_core(g, core, x, T, topo)
